import numpy as np, ml_dtypes
CORES = [71,199,95,223,103,231,111,239,119,247,127,255]
N = 12
T = 4096
def entries(a): return a.T.reshape(-1)
def pack(v, P): return np.ascontiguousarray(np.asarray(v, np.int32).reshape(-1, P).T)
def lists(rng, how):
    h = rng.integers(0, N * T, 8)
    if how == "zero": h[:] = 0
    if how == "blocks": h = T * rng.integers(1, N, 8)
    if how == "last": h[:] = N * T - 1
    if how == "mixed": h = T * rng.choice([q for q in range(N) if q & (q - 1)], 8) + rng.integers(1, T, 8)
    if how == "small": h = rng.integers(1, T, 8)
    h[1:] = 0
    return {"hh": np.broadcast_to(pack(np.concatenate([h, np.zeros(24, np.int64)]), 16), (N, 16, 2)).copy()}
def setup_inputs(rng):
    return dict({"x": rng.standard_normal((N, 128, T), dtype=np.float32).astype(ml_dtypes.bfloat16)}, **lists(rng, "uniform"))
def setup_inputs_blocks(rng):
    d = setup_inputs(rng); d.update(lists(rng, "blocks"))
    for k in ("x",): d[k] = (d[k].astype(np.float32) * 1048576.0).astype(d[k].dtype)
    return d
def setup_inputs_last(rng):
    d = setup_inputs(rng); d.update(lists(rng, "last"))
    for k in ("x",): d[k] = (d[k].astype(np.float32) * (1 / 1024.0)).astype(d[k].dtype)
    return d
def setup_inputs_mixed(rng):
    d = setup_inputs(rng); d.update(lists(rng, "mixed"))
    return d
def setup_inputs_small(rng):
    d = setup_inputs(rng); d.update(lists(rng, "small"))
    return d
def setup_inputs_zero(rng):
    d = setup_inputs(rng); d.update(lists(rng, "zero"))
    return d
def check_inputs(x):
    bad = []
    if x["hh"].min() < 0 or x["hh"].max() >= N * T: bad.append("hh out of range")
    if entries(x["hh"][0])[1:].any(): bad.append("an entry that should be 0 isn't")
    if not all(np.array_equal(a, x["hh"][0]) for a in x["hh"]): bad.append("hh isn't alike on all ranks")
    return bad
def reference(x, hh):
    h = entries(hh[0]); A = np.concatenate(list(x), axis=1)
    Y = np.roll(A, -int(h[0]), axis=1)
    return {"y": np.stack([Y[:, T * r:T * r + T] for r in range(N)])}

@@ -1,0 +1,237 @@
+from concourse.bass import DstId, RemoteDMATransfer
+from concourse.mybir import AluOpType, ActivationFunctionType
+
+N, COLS, WORLD = 12, 4096, 256
+WA, WB = 352, 160
+GROUP = 8
+NA = GROUP * WA
+KA = N * WA
+
+SCRATCH = {
+    "hb": ("sbuf", [16, 2], "int32"),
+    "hbc": ("sbuf", [128, 1], "int32"),
+    "hi": ("sbuf", [128, 2], "int32"),
+    "hf": ("sbuf", [128, 2], "float32"),
+    "qw": ("sbuf", [128, 1], "float32"),
+    "pi": ("sbuf", [128, 1], "int32"),
+    "pm": ("sbuf", [128, 1], "int32"),
+    "pf": ("sbuf", [128, 1], "float32"),
+    "base": ("sbuf", [128, KA // 16], "float32"),
+    "pos": ("sbuf", [128, KA // 16], "float32"),
+    "f1": ("sbuf", [128, KA // 16], "float32"),
+    "f2": ("sbuf", [128, KA // 16], "float32"),
+    "f3": ("sbuf", [128, KA // 16], "float32"),
+    "i1": ("sbuf", [128, COLS // 16], "int32"),
+    "i2": ("sbuf", [128, COLS // 16], "int32"),
+    "lst": ("sbuf", [128, KA // 16], "uint16"),
+    "xs": ("sbuf", [128, COLS], "bfloat16"),
+    "xr": ("sbuf", [128, COLS], "bfloat16"),
+    "z": ("sbuf", [128, COLS], "bfloat16"),
+    "slots": ("sbuf", [128, KA], "bfloat16"),
+    "res": ("sbuf", [128, KA], "bfloat16"),
+}
+SEMAPHORES = ["ldx", "ldh", "iot", "bc", "vq", "hrdy", "lrdy", "ca", "cb", "ls", "hr", "hm", "din", "za", "zb", "st"]
+
+
+def place(cores, topo):
+    used = {(topo.host(c), topo.chip(c)) for c in cores}
+    free = {}
+    for c in range(WORLD):
+        key = (topo.host(c), topo.chip(c))
+        if key in used or any(topo.mates(c, r) for r in cores):
+            continue
+        if all(topo.may_write(c, r) for r in cores):
+            free.setdefault(key, []).append(c)
+    pairs, seen = {}, set()
+    for key in sorted(free):
+        if key in seen:
+            continue
+        for other in sorted(free):
+            if topo.mates(free[key][0], free[other][0]):
+                a = [c for c in free[key] if topo.die(c) == 0][-1]
+                b = [c for c in free[other] if topo.die(c) == 1][-1]
+                pairs.setdefault(key[0], []).append((a, b))
+                seen.update((key, other))
+    order = []
+    for k in range(max(len(v) for v in pairs.values())):
+        for hst in sorted(pairs):
+            if k < len(pairs[hst]):
+                order.extend(pairs[hst][k])
+    return order[:2 * GROUP]
+
+
+def block(b):
+    return (b * WA, WA) if b < GROUP else (NA + (b - GROUP) * WB, WB)
+
+
+def engines(topo, src, dst):
+    m = topo.mask(src, dst)
+    return [1 << e for e in range(16) if (m >> e) & 1][:8]
+
+
+def send_list(b):
+    first = (3 * b) % N
+    return [((first + i) % N, 2 if i < 4 else 1) for i in range(N)]
+
+
+def transfer(topo, src, dst, engs, sem, s, d):
+    rid, pid = topo.addr(dst, src)
+    return RemoteDMATransfer(dst_ids=[DstId(rid=rid, pnc=pid)], dma_engine_mask=sum(engs), remote_sem=sem, srcs=[s], dsts=[d])
+
+
+def head_parts(mid):
+    return [(n % N, n) for n in range(len(mid))]
+
+
+def part_engines(mid, n):
+    return 8 // len([1 for r, m in head_parts(mid) if r == n % N])
+
+
+def rank_part(g, core, T, topo, mid, rank):
+    S, V, A = T.sem, g.vector, AluOpType
+    g.scalar.dma_start(T.hb[:], T.hh[:]).then_inc(S.ldh, 16)
+    g.sync.dma_start(T.xs[:], T.x[:]).then_inc(S.ldx, 16)
+
+    nc = COLS // 16
+    g.iota(T.pi[:], [[0, 1]], 0, 1).then_inc(S.iot, 1)
+    g.iota(T.i2[:], [[16, nc]], 0, 0).then_inc(S.iot, 1)
+    g.wait_ge(S.ldh, 16)
+    g.partition_broadcast(T.hbc[:], T.hb[0:1, 0:1], 128).then_inc(S.bc, 1)
+
+    V.wait_ge(S.iot, 2)
+    V.tensor_scalar(T.pm[:], T.pi[:], 15, None, A.bitwise_and).then_inc(S.vq, 1)
+    V.wait_ge(S.vq, 1)
+    V.tensor_copy(T.pf[:], T.pm[:]).then_inc(S.vq, 1)
+    V.wait_ge(S.vq, 2)
+    V.tensor_scalar(T.base[:, 0:nc], T.i2[:], T.pf[:], None, A.add).then_inc(S.vq, 1)
+    V.wait_ge(S.bc, 1)
+    V.tensor_scalar(T.hi[:, 1:2], T.hbc[:], COLS - 1, None, A.bitwise_and).then_inc(S.vq, 1)
+    V.tensor_scalar(T.hi[:, 0:1], T.hbc[:], 12, None, A.arith_shift_right).then_inc(S.vq, 1)
+    V.wait_ge(S.vq, 5)
+    V.tensor_copy(T.hf[:], T.hi[:]).then_inc(S.hrdy, 1)
+    V.wait_ge(S.hrdy, 1)
+    V.tensor_scalar(T.i1[:], T.base[:, 0:nc], T.hf[:, 1:2], None, A.add).then_inc(S.vq, 1)
+    V.wait_ge(S.vq, 6)
+    V.tensor_scalar(T.i2[:], T.i1[:], COLS - 1, None, A.bitwise_and).then_inc(S.vq, 1)
+    V.wait_ge(S.vq, 7)
+    V.tensor_copy(T.lst[:, 0:nc], T.i2[:]).then_inc(S.lrdy, 1)
+
+    ha, hb = NA // 2, NA + (COLS - NA) // 2
+    V.wait_ge(S.lrdy, 1)
+    V.wait_ge(S.ldx, 16)
+    g.scalar.wait_ge(S.lrdy, 1)
+    g.scalar.wait_ge(S.ldx, 16)
+    for lo, mi, hi, sem in ((0, ha, NA, S.ca), (NA, hb, COLS, S.cb)):
+        V.tensor_copy(T.xr[:, lo:mi], T.xs[:].indirect(T.lst[:, lo // 16:mi // 16])).then_inc(sem, 1)
+        g.scalar.activation(T.xr[:, mi:hi], T.xs[:].indirect(T.lst[:, mi // 16:hi // 16]),
+                            ActivationFunctionType.Copy, bias=-0.0).then_inc(sem, 1)
+
+    g.wait_ge(S.hrdy, 1)
+    tr = []
+    for r, n in head_parts(mid):
+        if r == rank:
+            k = part_engines(mid, n)
+            engs = engines(topo, core, mid[n])[len(tr) * k:(len(tr) + 1) * k]
+            col = n % 2
+            tr.append(transfer(topo, core, mid[n], engs, S.hr, T.hf[:, col:col + 1], T.hf[:, col:col + 1]))
+    g.remote_dma_fused(tr, local_sem=S.ls)
+
+    for first, sem in ((0, S.ca), (GROUP, S.cb)):
+        g.wait_ge(sem, 2)
+        tr = []
+        for i in range(GROUP):
+            b = first + i
+            c0, w = block(b)
+            tr.append(transfer(topo, core, mid[b], engines(topo, core, mid[b])[i:i + 1], S.din,
+                               T.xr[:, c0:c0 + w], T.slots[:, rank * w:(rank + 1) * w]))
+        g.remote_dma_fused(tr, local_sem=S.ls)
+
+    counts = [0, 0]
+    for b in range(2 * GROUP):
+        counts[b // GROUP] += dict(send_list(b))[rank]
+    g.sync.wait_ge(S.za, counts[0])
+    g.sync.dma_start(T.y[:, 0:NA], T.z[:, 0:NA]).then_inc(S.st, 16)
+    g.sync.wait_ge(S.zb, counts[1])
+    g.sync.dma_start(T.y[:, NA:COLS], T.z[:, NA:COLS]).then_inc(S.st, 16)
+    g.sync.wait_ge(S.st, 32)
+    g.wait_ge(S.ls, 24)
+
+
+def middle_part(g, core, T, topo, mid, b):
+    S, V, A = T.sem, g.vector, AluOpType
+    c0, w = block(b)
+    n, nc, wc = N * w, N * w // 16, w // 16
+    order = send_list(b)
+    first = order[0][0]
+    g.iota(T.pi[:], [[0, 1]], 0, 1).then_inc(S.iot, 1)
+    g.iota(T.f1[:, 0:(N - first) * wc], [[16, (N - first) * wc]], first * w, 0,
+           allow_small_or_imprecise_dtypes=True).then_inc(S.iot, 1)
+    k = 2
+    if first:
+        g.iota(T.f1[:, (N - first) * wc:nc], [[16, first * wc]], 0, 0,
+               allow_small_or_imprecise_dtypes=True).then_inc(S.iot, 1)
+        k += 1
+    g.iota(T.f2[:, 0:nc], [[0, N], [16, wc]], c0, 0, allow_small_or_imprecise_dtypes=True).then_inc(S.iot, 1)
+    k += 1
+
+    col = b % 2
+    peer = mid[b ^ 1]
+    cnt = part_engines(mid, b)
+    g.wait_ge(S.hr, cnt)
+    g.remote_dma_fused([transfer(topo, core, peer, engines(topo, core, peer), S.hm,
+                                 T.hf[:, col:col + 1], T.hf[:, col:col + 1])], local_sem=S.ls)
+
+    V.wait_ge(S.iot, k)
+    V.tensor_scalar(T.pm[:], T.pi[:], 15, None, A.bitwise_and).then_inc(S.vq, 1)
+    V.wait_ge(S.vq, 1)
+    V.tensor_copy(T.pf[:], T.pm[:]).then_inc(S.vq, 1)
+    V.wait_ge(S.vq, 2)
+    V.tensor_scalar(T.base[:, 0:nc], T.f1[:, 0:nc], T.pf[:], None, A.add).then_inc(S.vq, 1)
+    V.tensor_scalar(T.pos[:, 0:nc], T.f2[:, 0:nc], T.pf[:], None, A.add).then_inc(S.vq, 1)
+    V.wait_ge(S.vq, 4)
+    V.wait_ge(S.hr, cnt)
+    V.wait_ge(S.hm, 8)
+    V.tensor_scalar(T.qw[:], T.hf[:, 0:1], float(w), None, A.mult).then_inc(S.vq, 1)
+    V.tensor_scalar(T.f1[:, 0:nc], T.pos[:, 0:nc], T.hf[:, 1:2], float(COLS), A.add, A.is_ge).then_inc(S.vq, 1)
+    V.wait_ge(S.vq, 6)
+    V.tensor_scalar(T.f2[:, 0:nc], T.f1[:, 0:nc], float(w), T.qw[:], A.mult, A.add).then_inc(S.vq, 1)
+    V.wait_ge(S.vq, 7)
+    V.tensor_tensor(T.f3[:, 0:nc], T.f2[:, 0:nc], T.base[:, 0:nc], A.add).then_inc(S.vq, 1)
+    V.wait_ge(S.vq, 8)
+    V.tensor_scalar(T.f1[:, 0:nc], T.f3[:, 0:nc], float(n), float(-n), A.is_ge, A.mult).then_inc(S.vq, 1)
+    V.wait_ge(S.vq, 9)
+    V.tensor_tensor(T.f2[:, 0:nc], T.f3[:, 0:nc], T.f1[:, 0:nc], A.add).then_inc(S.vq, 1)
+    V.wait_ge(S.vq, 10)
+    V.tensor_copy(T.lst[:, 0:nc], T.f2[:, 0:nc]).then_inc(S.lrdy, 1)
+
+    V.wait_ge(S.lrdy, 1)
+    V.wait_ge(S.din, N)
+    g.scalar.wait_ge(S.lrdy, 1)
+    g.scalar.wait_ge(S.din, N)
+    win = T.slots[:, 0:n]
+    for lo, mi, hi, sem in ((0, 2, 4, S.ca), (4, 8, 12, S.cb)):
+        V.tensor_copy(T.res[:, lo * w:mi * w], win.indirect(T.lst[:, lo * wc:mi * wc])).then_inc(sem, 1)
+        g.scalar.activation(T.res[:, mi * w:hi * w], win.indirect(T.lst[:, mi * wc:hi * wc]),
+                            ActivationFunctionType.Copy, bias=-0.0).then_inc(sem, 1)
+
+    zsem = S.za if b < GROUP else S.zb
+    for lo, hi, sem in ((0, 4, S.ca), (4, 12, S.cb)):
+        g.wait_ge(sem, 2)
+        tr, e = [], 0
+        for i in range(lo, hi):
+            r, k = order[i]
+            dst = T.cores[r]
+            tr.append(transfer(topo, core, dst, engines(topo, core, dst)[e:e + k], zsem,
+                               T.res[:, i * w:(i + 1) * w], T.z[:, c0:c0 + w]))
+            e += k
+        g.remote_dma_fused(tr, local_sem=S.ls)
+    g.wait_ge(S.ls, 24)
+
+
+def rank_program(g, core, T, topo):
+    mid = place(T.cores, topo)
+    rank = T.rank_of(core)
+    if rank is not None:
+        rank_part(g, core, T, topo, mid, rank)
+    elif core in mid:
+        middle_part(g, core, T, topo, mid, mid.index(core))

@@ -2,10 +2,9 @@ from concourse.bass import DstId, RemoteDMATransfer
 from concourse.mybir import AluOpType, ActivationFunctionType
 
 N, COLS, WORLD = 12, 4096, 256
-WA, WB = 352, 160
-GROUP = 8
-NA = GROUP * WA
-KA = N * WA
+SETS = [(8, 1, 128, True), (8, 1, 288, False), (8, 1, 96, False)]
+SPLIT = [(4, 2), (8, 1)]
+KMAX = N * max(s[2] for s in SETS)
 
 SCRATCH = {
     "hb": ("sbuf", [16, 2], "int32"),
@@ -16,21 +15,22 @@ SCRATCH = {
     "pi": ("sbuf", [128, 1], "int32"),
     "pm": ("sbuf", [128, 1], "int32"),
     "pf": ("sbuf", [128, 1], "float32"),
-    "base": ("sbuf", [128, KA // 16], "float32"),
-    "pos": ("sbuf", [128, KA // 16], "float32"),
-    "f1": ("sbuf", [128, KA // 16], "float32"),
-    "f2": ("sbuf", [128, KA // 16], "float32"),
-    "f3": ("sbuf", [128, KA // 16], "float32"),
+    "base": ("sbuf", [128, 384], "float32"),
+    "pos": ("sbuf", [128, 384], "float32"),
+    "f1": ("sbuf", [128, 384], "float32"),
+    "f2": ("sbuf", [128, 384], "float32"),
+    "f3": ("sbuf", [128, 384], "float32"),
     "i1": ("sbuf", [128, COLS // 16], "int32"),
     "i2": ("sbuf", [128, COLS // 16], "int32"),
-    "lst": ("sbuf", [128, KA // 16], "uint16"),
+    "lst": ("sbuf", [128, 384], "uint16"),
     "xs": ("sbuf", [128, COLS], "bfloat16"),
     "xr": ("sbuf", [128, COLS], "bfloat16"),
     "z": ("sbuf", [128, COLS], "bfloat16"),
-    "slots": ("sbuf", [128, KA], "bfloat16"),
-    "res": ("sbuf", [128, KA], "bfloat16"),
+    "slots": ("sbuf", [128, KMAX], "bfloat16"),
+    "res": ("sbuf", [128, KMAX], "bfloat16"),
 }
-SEMAPHORES = ["ldx", "ldh", "iot", "bc", "vq", "hrdy", "lrdy", "ca", "cb", "ls", "hr", "hm", "din", "za", "zb", "st"]
+SEMAPHORES = (["ldx", "ldh", "iot", "bc", "vq", "hrdy", "lrdy", "ls", "hr", "hm", "din", "hop", "sta", "stb"]
+              + ["c%d" % k for k in range(4)] + ["z%d" % k for k in range(4)])
 
 
 def place(cores, topo):
@@ -48,30 +48,48 @@ def place(cores, topo):
             continue
         for other in sorted(free):
             if topo.mates(free[key][0], free[other][0]):
-                a = [c for c in free[key] if topo.die(c) == 0][-1]
-                b = [c for c in free[other] if topo.die(c) == 1][-1]
-                pairs.setdefault(key[0], []).append((a, b))
+                pick = [[c for c in free[ch] if topo.die(c) == d][-1] for ch, d in ((key, 0), (other, 1), (key, 1), (other, 0))]
+                pairs.setdefault(key[0], []).append(pick)
                 seen.update((key, other))
     order = []
     for k in range(max(len(v) for v in pairs.values())):
         for hst in sorted(pairs):
             if k < len(pairs[hst]):
-                order.extend(pairs[hst][k])
-    return order[:2 * GROUP]
+                order.append(pairs[hst][k])
+    own, shared = order[:4], order[4:8]
+    return [c for p in shared for c in p[:2]] + [c for p in own for c in p[:2]] + [c for p in shared for c in p[2:]]
 
 
-def block(b):
-    return (b * WA, WA) if b < GROUP else (NA + (b - GROUP) * WB, WB)
+def helper_of(rcore, mid, topo):
+    for c in range(WORLD):
+        if (topo.host(c), topo.chip(c)) == (topo.host(rcore), topo.chip(rcore)) and topo.die(c) != topo.die(rcore):
+            if all(topo.may_write(c, m) for m in mid):
+                return c
+
+
+def blocks():
+    out, c = [], 0
+    for i, (n, e, w, via) in enumerate(SETS):
+        for _ in range(n):
+            out.append((i, c, w))
+            c += w
+    return out
+
+
+def span(i):
+    cs = [(c, c + w) for j, c, w in blocks() if j == i]
+    return cs[0][0], cs[-1][1]
 
 
 def engines(topo, src, dst):
     m = topo.mask(src, dst)
-    return [1 << e for e in range(16) if (m >> e) & 1][:8]
+    return [1 << e for e in range(16) if (m >> e) & 1]
 
 
 def send_list(b):
     first = (3 * b) % N
-    return [((first + i) % N, 2 if i < 4 else 1) for i in range(N)]
+    es = [e for n, e in SPLIT for _ in range(n)]
+    return [((first + i) % N, es[i]) for i in range(N)]
 
 
 def transfer(topo, src, dst, engs, sem, s, d):
@@ -79,12 +97,15 @@ def transfer(topo, src, dst, engs, sem, s, d):
     return RemoteDMATransfer(dst_ids=[DstId(rid=rid, pnc=pid)], dma_engine_mask=sum(engs), remote_sem=sem, srcs=[s], dsts=[d])
 
 
-def head_parts(mid):
-    return [(n % N, n) for n in range(len(mid))]
-
-
-def part_engines(mid, n):
-    return 8 // len([1 for r, m in head_parts(mid) if r == n % N])
+def send_set(g, core, T, topo, mid, rank, i):
+    n, e, w, via = SETS[i]
+    tr = []
+    for b, (j, c0, _) in enumerate(blocks()):
+        if j == i:
+            es = engines(topo, core, mid[b])[len(tr) * e:(len(tr) + 1) * e]
+            tr.append(transfer(topo, core, mid[b], es, T.sem.din, T.xr[:, c0:c0 + w], T.slots[:, rank * w:(rank + 1) * w]))
+    g.remote_dma_fused(tr, local_sem=T.sem.ls)
+    return n * e
 
 
 def rank_part(g, core, T, topo, mid, rank):
@@ -116,50 +137,57 @@ def rank_part(g, core, T, topo, mid, rank):
     V.wait_ge(S.vq, 7)
     V.tensor_copy(T.lst[:, 0:nc], T.i2[:]).then_inc(S.lrdy, 1)
 
-    ha, hb = NA // 2, NA + (COLS - NA) // 2
     V.wait_ge(S.lrdy, 1)
     V.wait_ge(S.ldx, 16)
     g.scalar.wait_ge(S.lrdy, 1)
     g.scalar.wait_ge(S.ldx, 16)
-    for lo, mi, hi, sem in ((0, ha, NA, S.ca), (NA, hb, COLS, S.cb)):
-        V.tensor_copy(T.xr[:, lo:mi], T.xs[:].indirect(T.lst[:, lo // 16:mi // 16])).then_inc(sem, 1)
+    for i in range(len(SETS)):
+        lo, hi = span(i)
+        mi = (lo + hi) // 2
+        V.tensor_copy(T.xr[:, lo:mi], T.xs[:].indirect(T.lst[:, lo // 16:mi // 16])).then_inc(S["c%d" % i], 1)
         g.scalar.activation(T.xr[:, mi:hi], T.xs[:].indirect(T.lst[:, mi // 16:hi // 16]),
-                            ActivationFunctionType.Copy, bias=-0.0).then_inc(sem, 1)
+                            ActivationFunctionType.Copy, bias=-0.0).then_inc(S["c%d" % i], 1)
 
     g.wait_ge(S.hrdy, 1)
     tr = []
-    for r, n in head_parts(mid):
-        if r == rank:
-            k = part_engines(mid, n)
-            engs = engines(topo, core, mid[n])[len(tr) * k:(len(tr) + 1) * k]
-            col = n % 2
-            tr.append(transfer(topo, core, mid[n], engs, S.hr, T.hf[:, col:col + 1], T.hf[:, col:col + 1]))
+    for col in (0, 1):
+        m = mid[2 * rank + col]
+        tr.append(transfer(topo, core, m, engines(topo, core, m)[4 * col:4 * col + 4], S.hr, T.hf[:, col:col + 1], T.hf[:, col:col + 1]))
     g.remote_dma_fused(tr, local_sem=S.ls)
+    total = 8
 
-    for first, sem in ((0, S.ca), (GROUP, S.cb)):
-        g.wait_ge(sem, 2)
-        tr = []
-        for i in range(GROUP):
-            b = first + i
-            c0, w = block(b)
-            tr.append(transfer(topo, core, mid[b], engines(topo, core, mid[b])[i:i + 1], S.din,
-                               T.xr[:, c0:c0 + w], T.slots[:, rank * w:(rank + 1) * w]))
-        g.remote_dma_fused(tr, local_sem=S.ls)
+    help_core = helper_of(core, mid, topo)
+    for i, (n, e, w, via) in enumerate(SETS):
+        g.wait_ge(S["c%d" % i], 2)
+        if via:
+            off = engines(topo, core, mid[0])
+            es = [x for x in engines(topo, core, help_core) if x not in off]
+            lo, hi = span(i)
+            g.remote_dma_fused([transfer(topo, core, help_core, es, S.hop, T.xr[:, lo:hi], T.xr[:, lo:hi])], local_sem=S.ls)
+            total += len(es)
+        else:
+            total += send_set(g, core, T, topo, mid, rank, i)
 
-    counts = [0, 0]
-    for b in range(2 * GROUP):
-        counts[b // GROUP] += dict(send_list(b))[rank]
-    g.sync.wait_ge(S.za, counts[0])
-    g.sync.dma_start(T.y[:, 0:NA], T.z[:, 0:NA]).then_inc(S.st, 16)
-    g.sync.wait_ge(S.zb, counts[1])
-    g.sync.dma_start(T.y[:, NA:COLS], T.z[:, NA:COLS]).then_inc(S.st, 16)
-    g.sync.wait_ge(S.st, 32)
-    g.wait_ge(S.ls, 24)
+    for i in range(len(SETS)):
+        q, st = (g.scalar, S.stb) if i == 1 else (g.sync, S.sta)
+        q.wait_ge(S["z%d" % i], sum(dict(send_list(b))[rank] for b, (j, c0, w) in enumerate(blocks()) if j == i))
+        lo, hi = span(i)
+        q.dma_start(T.y[:, lo:hi], T.z[:, lo:hi]).then_inc(st, 16)
+    g.sync.wait_ge(S.sta, 32)
+    g.scalar.wait_ge(S.stb, 16)
+    g.wait_ge(S.ls, total)
+
+
+def helper_part(g, core, T, topo, mid, rank):
+    off = engines(topo, T.cores[rank], mid[0])
+    g.wait_ge(T.sem.hop, len([x for x in engines(topo, T.cores[rank], core) if x not in off]))
+    total = sum(send_set(g, core, T, topo, mid, rank, i) for i in range(len(SETS)) if SETS[i][3])
+    g.wait_ge(T.sem.ls, total)
 
 
 def middle_part(g, core, T, topo, mid, b):
     S, V, A = T.sem, g.vector, AluOpType
-    c0, w = block(b)
+    i, c0, w = blocks()[b]
     n, nc, wc = N * w, N * w // 16, w // 16
     order = send_list(b)
     first = order[0][0]
@@ -176,8 +204,7 @@ def middle_part(g, core, T, topo, mid, b):
 
     col = b % 2
     peer = mid[b ^ 1]
-    cnt = part_engines(mid, b)
-    g.wait_ge(S.hr, cnt)
+    g.wait_ge(S.hr, 4)
     g.remote_dma_fused([transfer(topo, core, peer, engines(topo, core, peer), S.hm,
                                  T.hf[:, col:col + 1], T.hf[:, col:col + 1])], local_sem=S.ls)
 
@@ -189,8 +216,8 @@ def middle_part(g, core, T, topo, mid, b):
     V.tensor_scalar(T.base[:, 0:nc], T.f1[:, 0:nc], T.pf[:], None, A.add).then_inc(S.vq, 1)
     V.tensor_scalar(T.pos[:, 0:nc], T.f2[:, 0:nc], T.pf[:], None, A.add).then_inc(S.vq, 1)
     V.wait_ge(S.vq, 4)
-    V.wait_ge(S.hr, cnt)
-    V.wait_ge(S.hm, 8)
+    V.wait_ge(S.hr, 4)
+    V.wait_ge(S.hm, len(engines(topo, peer, core)))
     V.tensor_scalar(T.qw[:], T.hf[:, 0:1], float(w), None, A.mult).then_inc(S.vq, 1)
     V.tensor_scalar(T.f1[:, 0:nc], T.pos[:, 0:nc], T.hf[:, 1:2], float(COLS), A.add, A.is_ge).then_inc(S.vq, 1)
     V.wait_ge(S.vq, 6)
@@ -204,28 +231,28 @@ def middle_part(g, core, T, topo, mid, b):
     V.wait_ge(S.vq, 10)
     V.tensor_copy(T.lst[:, 0:nc], T.f2[:, 0:nc]).then_inc(S.lrdy, 1)
 
+    got = N * SETS[i][1]
     V.wait_ge(S.lrdy, 1)
-    V.wait_ge(S.din, N)
+    V.wait_ge(S.din, got)
     g.scalar.wait_ge(S.lrdy, 1)
-    g.scalar.wait_ge(S.din, N)
+    g.scalar.wait_ge(S.din, got)
     win = T.slots[:, 0:n]
-    for lo, mi, hi, sem in ((0, 2, 4, S.ca), (4, 8, 12, S.cb)):
-        V.tensor_copy(T.res[:, lo * w:mi * w], win.indirect(T.lst[:, lo * wc:mi * wc])).then_inc(sem, 1)
+    lo = 0
+    for k, (m, e) in enumerate(SPLIT):
+        mi, hi = lo + m // 2, lo + m
+        V.tensor_copy(T.res[:, lo * w:mi * w], win.indirect(T.lst[:, lo * wc:mi * wc])).then_inc(S["c%d" % k], 1)
         g.scalar.activation(T.res[:, mi * w:hi * w], win.indirect(T.lst[:, mi * wc:hi * wc]),
-                            ActivationFunctionType.Copy, bias=-0.0).then_inc(sem, 1)
-
-    zsem = S.za if b < GROUP else S.zb
-    for lo, hi, sem in ((0, 4, S.ca), (4, 12, S.cb)):
-        g.wait_ge(sem, 2)
-        tr, e = [], 0
-        for i in range(lo, hi):
-            r, k = order[i]
+                            ActivationFunctionType.Copy, bias=-0.0).then_inc(S["c%d" % k], 1)
+        g.wait_ge(S["c%d" % k], 2)
+        tr = []
+        for t in range(lo, hi):
+            r, e = order[t]
             dst = T.cores[r]
-            tr.append(transfer(topo, core, dst, engines(topo, core, dst)[e:e + k], zsem,
-                               T.res[:, i * w:(i + 1) * w], T.z[:, c0:c0 + w]))
-            e += k
+            tr.append(transfer(topo, core, dst, engines(topo, core, dst)[len(tr) * e:(len(tr) + 1) * e], S["z%d" % i],
+                               T.res[:, t * w:(t + 1) * w], T.z[:, c0:c0 + w]))
         g.remote_dma_fused(tr, local_sem=S.ls)
-    g.wait_ge(S.ls, 24)
+        lo = hi
+    g.wait_ge(S.ls, len(engines(topo, core, peer)) + sum(m * e for m, e in SPLIT))
 
 
 def rank_program(g, core, T, topo):
@@ -235,3 +262,7 @@ def rank_program(g, core, T, topo):
         rank_part(g, core, T, topo, mid, rank)
     elif core in mid:
         middle_part(g, core, T, topo, mid, mid.index(core))
+    else:
+        helpers = [helper_of(r, mid, topo) for r in T.cores]
+        if core in helpers:
+            helper_part(g, core, T, topo, mid, helpers.index(core))

@@ -2,7 +2,8 @@ from concourse.bass import DstId, RemoteDMATransfer
 from concourse.mybir import AluOpType, ActivationFunctionType
 
 N, COLS, WORLD = 12, 4096, 256
-SETS = [(8, 1, 128, True), (8, 1, 288, False), (8, 1, 96, False)]
+SETS = [(8, 1, 128, 0), (8, 1, 192, None), (8, 1, 96, 1), (8, 1, 96, None)]
+HELPERS = 2
 SPLIT = [(4, 2), (8, 1)]
 KMAX = N * max(s[2] for s in SETS)
 
@@ -11,25 +12,26 @@ SCRATCH = {
     "hbc": ("sbuf", [128, 1], "int32"),
     "hi": ("sbuf", [128, 2], "int32"),
     "hf": ("sbuf", [128, 2], "float32"),
+    "hw": ("sbuf", [128, 1], "float32"),
     "qw": ("sbuf", [128, 1], "float32"),
     "pi": ("sbuf", [128, 1], "int32"),
     "pm": ("sbuf", [128, 1], "int32"),
     "pf": ("sbuf", [128, 1], "float32"),
-    "base": ("sbuf", [128, 384], "float32"),
-    "pos": ("sbuf", [128, 384], "float32"),
-    "f1": ("sbuf", [128, 384], "float32"),
-    "f2": ("sbuf", [128, 384], "float32"),
-    "f3": ("sbuf", [128, 384], "float32"),
-    "i1": ("sbuf", [128, COLS // 16], "int32"),
-    "i2": ("sbuf", [128, COLS // 16], "int32"),
-    "lst": ("sbuf", [128, 384], "uint16"),
+    "base": ("sbuf", [128, 256], "float32"),
+    "pos": ("sbuf", [128, 256], "float32"),
+    "f1": ("sbuf", [128, 256], "float32"),
+    "f2": ("sbuf", [128, 256], "float32"),
+    "f3": ("sbuf", [128, 256], "float32"),
+    "i1": ("sbuf", [128, 256], "int32"),
+    "i2": ("sbuf", [128, 256], "int32"),
+    "lst": ("sbuf", [128, 256], "uint16"),
     "xs": ("sbuf", [128, COLS], "bfloat16"),
     "xr": ("sbuf", [128, COLS], "bfloat16"),
     "z": ("sbuf", [128, COLS], "bfloat16"),
     "slots": ("sbuf", [128, KMAX], "bfloat16"),
     "res": ("sbuf", [128, KMAX], "bfloat16"),
 }
-SEMAPHORES = (["ldx", "ldh", "iot", "bc", "vq", "hrdy", "lrdy", "ls", "hr", "hm", "din", "hop", "sta", "stb"]
+SEMAPHORES = (["ldx", "ldh", "iot", "bc", "vq", "hrdy", "la", "lb", "ls", "hr", "hm", "din", "hop", "sta", "stb"]
               + ["c%d" % k for k in range(4)] + ["z%d" % k for k in range(4)])
 
 
@@ -56,15 +58,18 @@ def place(cores, topo):
         for hst in sorted(pairs):
             if k < len(pairs[hst]):
                 order.append(pairs[hst][k])
-    own, shared = order[:4], order[4:8]
-    return [c for p in shared for c in p[:2]] + [c for p in own for c in p[:2]] + [c for p in shared for c in p[2:]]
+    half, rest = order[4:8], order[:4]
+    return ([c for p in half for c in p[:2]] + [c for p in rest for c in p[:2]]
+            + [c for p in rest for c in p[2:]] + [c for p in half for c in p[2:]])
 
 
-def helper_of(rcore, mid, topo):
+def helpers_of(rcore, mid, topo):
+    out = []
     for c in range(WORLD):
         if (topo.host(c), topo.chip(c)) == (topo.host(rcore), topo.chip(rcore)) and topo.die(c) != topo.die(rcore):
             if all(topo.may_write(c, m) for m in mid):
-                return c
+                out.append(c)
+    return out[:HELPERS]
 
 
 def blocks():
@@ -97,6 +102,10 @@ def transfer(topo, src, dst, engs, sem, s, d):
     return RemoteDMATransfer(dst_ids=[DstId(rid=rid, pnc=pid)], dma_engine_mask=sum(engs), remote_sem=sem, srcs=[s], dsts=[d])
 
 
+def parts_of(rank, mid):
+    return [n for n in range(len(mid)) if (n // 2) % N == rank]
+
+
 def send_set(g, core, T, topo, mid, rank, i):
     n, e, w, via = SETS[i]
     tr = []
@@ -124,24 +133,31 @@ def rank_part(g, core, T, topo, mid, rank):
     V.wait_ge(S.vq, 1)
     V.tensor_copy(T.pf[:], T.pm[:]).then_inc(S.vq, 1)
     V.wait_ge(S.vq, 2)
-    V.tensor_scalar(T.base[:, 0:nc], T.i2[:], T.pf[:], None, A.add).then_inc(S.vq, 1)
+    V.tensor_scalar(T.base[:], T.i2[:], T.pf[:], None, A.add).then_inc(S.vq, 1)
     V.wait_ge(S.bc, 1)
     V.tensor_scalar(T.hi[:, 1:2], T.hbc[:], COLS - 1, None, A.bitwise_and).then_inc(S.vq, 1)
     V.tensor_scalar(T.hi[:, 0:1], T.hbc[:], 12, None, A.arith_shift_right).then_inc(S.vq, 1)
-    V.wait_ge(S.vq, 5)
-    V.tensor_copy(T.hf[:], T.hi[:]).then_inc(S.hrdy, 1)
-    V.wait_ge(S.hrdy, 1)
-    V.tensor_scalar(T.i1[:], T.base[:, 0:nc], T.hf[:, 1:2], None, A.add).then_inc(S.vq, 1)
+    V.tensor_copy(T.hw[:], T.hbc[:]).then_inc(S.vq, 1)
     V.wait_ge(S.vq, 6)
-    V.tensor_scalar(T.i2[:], T.i1[:], COLS - 1, None, A.bitwise_and).then_inc(S.vq, 1)
-    V.wait_ge(S.vq, 7)
-    V.tensor_copy(T.lst[:, 0:nc], T.i2[:]).then_inc(S.lrdy, 1)
+    V.tensor_copy(T.hf[:], T.hi[:]).then_inc(S.hrdy, 1)
+    cut = span(0)[1] // 16
+    two = ((0, cut), (cut, nc))
+    for a, z in two:
+        V.tensor_scalar(T.i1[:, a:z], T.base[:, a:z], T.hw[:], None, A.add).then_inc(S.vq, 1)
+    V.wait_ge(S.vq, 8)
+    for a, z in two:
+        V.tensor_scalar(T.i2[:, a:z], T.i1[:, a:z], COLS - 1, None, A.bitwise_and).then_inc(S.vq, 1)
+    V.wait_ge(S.vq, 10)
+    for (a, z), sem in zip(two, (S.la, S.lb)):
+        V.tensor_copy(T.lst[:, a:z], T.i2[:, a:z]).then_inc(sem, 1)
 
-    V.wait_ge(S.lrdy, 1)
-    V.wait_ge(S.ldx, 16)
-    g.scalar.wait_ge(S.lrdy, 1)
-    g.scalar.wait_ge(S.ldx, 16)
+    for q in (V, g.scalar):
+        q.wait_ge(S.la, 1)
+        q.wait_ge(S.ldx, 16)
     for i in range(len(SETS)):
+        if i == 1:
+            V.wait_ge(S.lb, 1)
+            g.scalar.wait_ge(S.lb, 1)
         lo, hi = span(i)
         mi = (lo + hi) // 2
         V.tensor_copy(T.xr[:, lo:mi], T.xs[:].indirect(T.lst[:, lo // 16:mi // 16])).then_inc(S["c%d" % i], 1)
@@ -149,39 +165,41 @@ def rank_part(g, core, T, topo, mid, rank):
                             ActivationFunctionType.Copy, bias=-0.0).then_inc(S["c%d" % i], 1)
 
     g.wait_ge(S.hrdy, 1)
-    tr = []
-    for col in (0, 1):
-        m = mid[2 * rank + col]
-        tr.append(transfer(topo, core, m, engines(topo, core, m)[4 * col:4 * col + 4], S.hr, T.hf[:, col:col + 1], T.hf[:, col:col + 1]))
+    tr, mine = [], parts_of(rank, mid)
+    k = 8 // len(mine)
+    for n in mine:
+        es = engines(topo, core, mid[n])[len(tr) * k:(len(tr) + 1) * k]
+        col = n % 2
+        tr.append(transfer(topo, core, mid[n], es, S.hr, T.hf[:, col:col + 1], T.hf[:, col:col + 1]))
     g.remote_dma_fused(tr, local_sem=S.ls)
     total = 8
 
-    help_core = helper_of(core, mid, topo)
+    helpers = helpers_of(core, mid, topo)
+    off = engines(topo, core, mid[0])
     for i, (n, e, w, via) in enumerate(SETS):
         g.wait_ge(S["c%d" % i], 2)
-        if via:
-            off = engines(topo, core, mid[0])
-            es = [x for x in engines(topo, core, help_core) if x not in off]
-            lo, hi = span(i)
-            g.remote_dma_fused([transfer(topo, core, help_core, es, S.hop, T.xr[:, lo:hi], T.xr[:, lo:hi])], local_sem=S.ls)
-            total += len(es)
-        else:
+        if via is None:
             total += send_set(g, core, T, topo, mid, rank, i)
+        else:
+            es = [x for x in engines(topo, core, helpers[via]) if x not in off]
+            lo, hi = span(i)
+            g.remote_dma_fused([transfer(topo, core, helpers[via], es, S.hop, T.xr[:, lo:hi], T.xr[:, lo:hi])], local_sem=S.ls)
+            total += len(es)
 
     for i in range(len(SETS)):
-        q, st = (g.scalar, S.stb) if i == 1 else (g.sync, S.sta)
+        q, st = (g.scalar, S.stb) if i % 2 else (g.sync, S.sta)
         q.wait_ge(S["z%d" % i], sum(dict(send_list(b))[rank] for b, (j, c0, w) in enumerate(blocks()) if j == i))
         lo, hi = span(i)
         q.dma_start(T.y[:, lo:hi], T.z[:, lo:hi]).then_inc(st, 16)
     g.sync.wait_ge(S.sta, 32)
-    g.scalar.wait_ge(S.stb, 16)
+    g.scalar.wait_ge(S.stb, 32)
     g.wait_ge(S.ls, total)
 
 
-def helper_part(g, core, T, topo, mid, rank):
+def helper_part(g, core, T, topo, mid, rank, k):
     off = engines(topo, T.cores[rank], mid[0])
     g.wait_ge(T.sem.hop, len([x for x in engines(topo, T.cores[rank], core) if x not in off]))
-    total = sum(send_set(g, core, T, topo, mid, rank, i) for i in range(len(SETS)) if SETS[i][3])
+    total = sum(send_set(g, core, T, topo, mid, rank, i) for i in range(len(SETS)) if SETS[i][3] == k)
     g.wait_ge(T.sem.ls, total)
 
 
@@ -204,38 +222,52 @@ def middle_part(g, core, T, topo, mid, b):
 
     col = b % 2
     peer = mid[b ^ 1]
-    g.wait_ge(S.hr, 4)
+    direct = 8 // len(parts_of((b // 2) % N, mid))
+    g.wait_ge(S.hr, direct)
     g.remote_dma_fused([transfer(topo, core, peer, engines(topo, core, peer), S.hm,
                                  T.hf[:, col:col + 1], T.hf[:, col:col + 1])], local_sem=S.ls)
 
+    base, pos, f1, f2, f3 = (t[:, 0:nc] for t in (T.base, T.pos, T.f1, T.f2, T.f3))
+    q, s = T.hf[:, 0:1], T.hf[:, 1:2]
+    count = [0]
+
+    def step(ins):
+        ins.then_inc(S.vq, 1)
+        count[0] += 1
+        V.wait_ge(S.vq, count[0])
+
     V.wait_ge(S.iot, k)
-    V.tensor_scalar(T.pm[:], T.pi[:], 15, None, A.bitwise_and).then_inc(S.vq, 1)
-    V.wait_ge(S.vq, 1)
-    V.tensor_copy(T.pf[:], T.pm[:]).then_inc(S.vq, 1)
-    V.wait_ge(S.vq, 2)
-    V.tensor_scalar(T.base[:, 0:nc], T.f1[:, 0:nc], T.pf[:], None, A.add).then_inc(S.vq, 1)
-    V.tensor_scalar(T.pos[:, 0:nc], T.f2[:, 0:nc], T.pf[:], None, A.add).then_inc(S.vq, 1)
-    V.wait_ge(S.vq, 4)
-    V.wait_ge(S.hr, 4)
-    V.wait_ge(S.hm, len(engines(topo, peer, core)))
-    V.tensor_scalar(T.qw[:], T.hf[:, 0:1], float(w), None, A.mult).then_inc(S.vq, 1)
-    V.tensor_scalar(T.f1[:, 0:nc], T.pos[:, 0:nc], T.hf[:, 1:2], float(COLS), A.add, A.is_ge).then_inc(S.vq, 1)
-    V.wait_ge(S.vq, 6)
-    V.tensor_scalar(T.f2[:, 0:nc], T.f1[:, 0:nc], float(w), T.qw[:], A.mult, A.add).then_inc(S.vq, 1)
-    V.wait_ge(S.vq, 7)
-    V.tensor_tensor(T.f3[:, 0:nc], T.f2[:, 0:nc], T.base[:, 0:nc], A.add).then_inc(S.vq, 1)
-    V.wait_ge(S.vq, 8)
-    V.tensor_scalar(T.f1[:, 0:nc], T.f3[:, 0:nc], float(n), float(-n), A.is_ge, A.mult).then_inc(S.vq, 1)
-    V.wait_ge(S.vq, 9)
-    V.tensor_tensor(T.f2[:, 0:nc], T.f3[:, 0:nc], T.f1[:, 0:nc], A.add).then_inc(S.vq, 1)
-    V.wait_ge(S.vq, 10)
-    V.tensor_copy(T.lst[:, 0:nc], T.f2[:, 0:nc]).then_inc(S.lrdy, 1)
+    step(V.tensor_scalar(T.pm[:], T.pi[:], 15, None, A.bitwise_and))
+    step(V.tensor_copy(T.pf[:], T.pm[:]))
+    step(V.tensor_scalar(base, f1, T.pf[:], None, A.add))
+    step(V.tensor_scalar(pos, f2, T.pf[:], None, A.add))
+    V.wait_ge(S.hr, direct)
+    if col == 0:
+        step(V.tensor_scalar(T.qw[:], q, float(w), None, A.mult))
+        step(V.tensor_scalar(f1, base, T.qw[:], None, A.add))
+        step(V.tensor_scalar(f2, f1, float(n), float(-n), A.is_ge, A.mult))
+        step(V.tensor_tensor(f3, f1, f2, A.add))
+        step(V.tensor_scalar(f1, f3, float(n - w), float(-n), A.is_ge, A.mult))
+        step(V.tensor_scalar(base, f1, float(w), None, A.add))
+        V.wait_ge(S.hm, len(engines(topo, peer, core)))
+        step(V.tensor_scalar(f2, pos, s, float(COLS), A.add, A.is_ge))
+        step(V.tensor_tensor(f1, f2, base, A.mult))
+        step(V.tensor_tensor(pos, f1, f3, A.add))
+    else:
+        step(V.tensor_scalar(f1, pos, s, float(COLS), A.add, A.is_ge))
+        step(V.tensor_scalar(f2, f1, float(w), None, A.mult))
+        step(V.tensor_tensor(f3, base, f2, A.add))
+        V.wait_ge(S.hm, len(engines(topo, peer, core)))
+        step(V.tensor_scalar(T.qw[:], q, float(w), None, A.mult))
+        step(V.tensor_scalar(f1, f3, T.qw[:], None, A.add))
+        step(V.tensor_scalar(f2, f1, float(n), float(-n), A.is_ge, A.mult))
+        step(V.tensor_tensor(pos, f1, f2, A.add))
+    V.tensor_copy(T.lst[:, 0:nc], pos).then_inc(S.la, 1)
 
     got = N * SETS[i][1]
-    V.wait_ge(S.lrdy, 1)
-    V.wait_ge(S.din, got)
-    g.scalar.wait_ge(S.lrdy, 1)
-    g.scalar.wait_ge(S.din, got)
+    for qu in (V, g.scalar):
+        qu.wait_ge(S.la, 1)
+        qu.wait_ge(S.din, got)
     win = T.slots[:, 0:n]
     lo = 0
     for k, (m, e) in enumerate(SPLIT):
@@ -263,6 +295,7 @@ def rank_program(g, core, T, topo):
     elif core in mid:
         middle_part(g, core, T, topo, mid, mid.index(core))
     else:
-        helpers = [helper_of(r, mid, topo) for r in T.cores]
-        if core in helpers:
-            helper_part(g, core, T, topo, mid, helpers.index(core))
+        for r, rcore in enumerate(T.cores):
+            helpers = helpers_of(rcore, mid, topo)
+            if core in helpers:
+                helper_part(g, core, T, topo, mid, r, helpers.index(core))

@@ -2,9 +2,9 @@ from concourse.bass import DstId, RemoteDMATransfer
 from concourse.mybir import AluOpType, ActivationFunctionType
 
 N, COLS, WORLD = 12, 4096, 256
-SETS = [(8, 1, 128, 0), (8, 1, 192, None), (8, 1, 96, 1), (8, 1, 96, None)]
-HELPERS = 2
+SETS = [(8, 1, 64, 0), (8, 1, 128, None), (8, 1, 80, 1), (8, 1, 80, 2), (8, 1, 64, 0), (8, 1, 96, None)]
 SPLIT = [(4, 2), (8, 1)]
+STORES = [("sync", 0, 2), ("scalar", 2, 4), ("sync", 4, 5), ("scalar", 5, 6)]
 KMAX = N * max(s[2] for s in SETS)
 
 SCRATCH = {
@@ -31,8 +31,8 @@ SCRATCH = {
     "slots": ("sbuf", [128, KMAX], "bfloat16"),
     "res": ("sbuf", [128, KMAX], "bfloat16"),
 }
-SEMAPHORES = (["ldx", "ldh", "iot", "bc", "vq", "hrdy", "la", "lb", "ls", "hr", "hm", "din", "hop", "sta", "stb"]
-              + ["c%d" % k for k in range(4)] + ["z%d" % k for k in range(4)])
+SEMAPHORES = (["ldx", "ldh", "iot", "bc", "vq", "hrdy", "la", "lb", "ls", "hr", "hm", "din", "sta", "stb"]
+              + ["c%d" % k for k in range(6)] + ["z%d" % k for k in range(6)] + ["hop%d" % k for k in range(6)])
 
 
 def place(cores, topo):
@@ -50,8 +50,8 @@ def place(cores, topo):
             continue
         for other in sorted(free):
             if topo.mates(free[key][0], free[other][0]):
-                pick = [[c for c in free[ch] if topo.die(c) == d][-1] for ch, d in ((key, 0), (other, 1), (key, 1), (other, 0))]
-                pairs.setdefault(key[0], []).append(pick)
+                on = {(ch, d): [c for c in free[ch] if topo.die(c) == d] for ch in (key, other) for d in (0, 1)}
+                pairs.setdefault(key[0], []).append([(on[key, d][k], on[other, 1 - d][k]) for k in (-1, -2) for d in (0, 1)])
                 seen.update((key, other))
     order = []
     for k in range(max(len(v) for v in pairs.values())):
@@ -59,17 +59,17 @@ def place(cores, topo):
             if k < len(pairs[hst]):
                 order.append(pairs[hst][k])
     half, rest = order[4:8], order[:4]
-    return ([c for p in half for c in p[:2]] + [c for p in rest for c in p[:2]]
-            + [c for p in rest for c in p[2:]] + [c for p in half for c in p[2:]])
+    use = [(half, 0), (rest, 0), (rest, 1), (half, 1), (half, 2), (rest, 2)]
+    return [c for chips, k in use for p in chips for c in p[k]]
 
 
 def helpers_of(rcore, mid, topo):
-    out = []
+    near, far = [], []
     for c in range(WORLD):
-        if (topo.host(c), topo.chip(c)) == (topo.host(rcore), topo.chip(rcore)) and topo.die(c) != topo.die(rcore):
+        if c != rcore and (topo.host(c), topo.chip(c)) == (topo.host(rcore), topo.chip(rcore)):
             if all(topo.may_write(c, m) for m in mid):
-                out.append(c)
-    return out[:HELPERS]
+                (near if topo.die(c) == topo.die(rcore) else far).append(c)
+    return far[:2] + near[:1]
 
 
 def blocks():
@@ -183,13 +183,15 @@ def rank_part(g, core, T, topo, mid, rank):
         else:
             es = [x for x in engines(topo, core, helpers[via]) if x not in off]
             lo, hi = span(i)
-            g.remote_dma_fused([transfer(topo, core, helpers[via], es, S.hop, T.xr[:, lo:hi], T.xr[:, lo:hi])], local_sem=S.ls)
+            g.remote_dma_fused([transfer(topo, core, helpers[via], es, S["hop%d" % i], T.xr[:, lo:hi], T.xr[:, lo:hi])],
+                               local_sem=S.ls)
             total += len(es)
 
-    for i in range(len(SETS)):
-        q, st = (g.scalar, S.stb) if i % 2 else (g.sync, S.sta)
-        q.wait_ge(S["z%d" % i], sum(dict(send_list(b))[rank] for b, (j, c0, w) in enumerate(blocks()) if j == i))
-        lo, hi = span(i)
+    for name, first, last in STORES:
+        q, st = (g.scalar, S.stb) if name == "scalar" else (g.sync, S.sta)
+        for i in range(first, last):
+            q.wait_ge(S["z%d" % i], sum(dict(send_list(b))[rank] for b, (j, c0, w) in enumerate(blocks()) if j == i))
+        lo, hi = span(first)[0], span(last - 1)[1]
         q.dma_start(T.y[:, lo:hi], T.z[:, lo:hi]).then_inc(st, 16)
     g.sync.wait_ge(S.sta, 32)
     g.scalar.wait_ge(S.stb, 32)
@@ -198,8 +200,12 @@ def rank_part(g, core, T, topo, mid, rank):
 
 def helper_part(g, core, T, topo, mid, rank, k):
     off = engines(topo, T.cores[rank], mid[0])
-    g.wait_ge(T.sem.hop, len([x for x in engines(topo, T.cores[rank], core) if x not in off]))
-    total = sum(send_set(g, core, T, topo, mid, rank, i) for i in range(len(SETS)) if SETS[i][3] == k)
+    es = [x for x in engines(topo, T.cores[rank], core) if x not in off]
+    total = 0
+    for i in range(len(SETS)):
+        if SETS[i][3] == k:
+            g.wait_ge(T.sem["hop%d" % i], len(es))
+            total += send_set(g, core, T, topo, mid, rank, i)
     g.wait_ge(T.sem.ls, total)
 
 

from concourse.bass import DstId, RemoteDMATransfer
from concourse.mybir import AluOpType, ActivationFunctionType

N, COLS, WORLD = 12, 4096, 256
SETS = [(8, 1, 64, 0), (8, 1, 128, None), (8, 1, 80, 1), (8, 1, 80, 2), (8, 1, 64, 0), (8, 1, 96, None)]
SPLIT = [(4, 2), (8, 1)]
STORES = [("sync", 0, 2), ("scalar", 2, 4), ("sync", 4, 5), ("scalar", 5, 6)]
KMAX = N * max(s[2] for s in SETS)

SCRATCH = {
    "hb": ("sbuf", [16, 2], "int32"),
    "hbc": ("sbuf", [128, 1], "int32"),
    "hi": ("sbuf", [128, 2], "int32"),
    "hf": ("sbuf", [128, 2], "float32"),
    "hw": ("sbuf", [128, 1], "float32"),
    "qw": ("sbuf", [128, 1], "float32"),
    "pi": ("sbuf", [128, 1], "int32"),
    "pm": ("sbuf", [128, 1], "int32"),
    "pf": ("sbuf", [128, 1], "float32"),
    "base": ("sbuf", [128, 256], "float32"),
    "pos": ("sbuf", [128, 256], "float32"),
    "f1": ("sbuf", [128, 256], "float32"),
    "f2": ("sbuf", [128, 256], "float32"),
    "f3": ("sbuf", [128, 256], "float32"),
    "i1": ("sbuf", [128, 256], "int32"),
    "i2": ("sbuf", [128, 256], "int32"),
    "lst": ("sbuf", [128, 256], "uint16"),
    "xs": ("sbuf", [128, COLS], "bfloat16"),
    "xr": ("sbuf", [128, COLS], "bfloat16"),
    "z": ("sbuf", [128, COLS], "bfloat16"),
    "slots": ("sbuf", [128, KMAX], "bfloat16"),
    "res": ("sbuf", [128, KMAX], "bfloat16"),
}
SEMAPHORES = (["ldx", "ldh", "iot", "bc", "vq", "hrdy", "la", "lb", "ls", "hr", "hm", "din", "sta", "stb"]
              + ["c%d" % k for k in range(6)] + ["z%d" % k for k in range(6)] + ["hop%d" % k for k in range(6)])


def place(cores, topo):
    used = {(topo.host(c), topo.chip(c)) for c in cores}
    free = {}
    for c in range(WORLD):
        key = (topo.host(c), topo.chip(c))
        if key in used or any(topo.mates(c, r) for r in cores):
            continue
        if all(topo.may_write(c, r) for r in cores):
            free.setdefault(key, []).append(c)
    pairs, seen = {}, set()
    for key in sorted(free):
        if key in seen:
            continue
        for other in sorted(free):
            if topo.mates(free[key][0], free[other][0]):
                on = {(ch, d): [c for c in free[ch] if topo.die(c) == d] for ch in (key, other) for d in (0, 1)}
                pairs.setdefault(key[0], []).append([(on[key, d][k], on[other, 1 - d][k]) for k in (-1, -2) for d in (0, 1)])
                seen.update((key, other))
    order = []
    for k in range(max(len(v) for v in pairs.values())):
        for hst in sorted(pairs):
            if k < len(pairs[hst]):
                order.append(pairs[hst][k])
    half, rest = order[4:8], order[:4]
    use = [(half, 0), (rest, 0), (rest, 1), (half, 1), (half, 2), (rest, 2)]
    return [c for chips, k in use for p in chips for c in p[k]]


def helpers_of(rcore, mid, topo):
    near, far = [], []
    for c in range(WORLD):
        if c != rcore and (topo.host(c), topo.chip(c)) == (topo.host(rcore), topo.chip(rcore)):
            if all(topo.may_write(c, m) for m in mid):
                (near if topo.die(c) == topo.die(rcore) else far).append(c)
    return far[:2] + near[:1]


def blocks():
    out, c = [], 0
    for i, (n, e, w, via) in enumerate(SETS):
        for _ in range(n):
            out.append((i, c, w))
            c += w
    return out


def span(i):
    cs = [(c, c + w) for j, c, w in blocks() if j == i]
    return cs[0][0], cs[-1][1]


def engines(topo, src, dst):
    m = topo.mask(src, dst)
    return [1 << e for e in range(16) if (m >> e) & 1]


def send_list(b):
    first = (3 * b) % N
    es = [e for n, e in SPLIT for _ in range(n)]
    return [((first + i) % N, es[i]) for i in range(N)]


def transfer(topo, src, dst, engs, sem, s, d):
    rid, pid = topo.addr(dst, src)
    return RemoteDMATransfer(dst_ids=[DstId(rid=rid, pnc=pid)], dma_engine_mask=sum(engs), remote_sem=sem, srcs=[s], dsts=[d])


def parts_of(rank, mid):
    return [n for n in range(len(mid)) if (n // 2) % N == rank]


def send_set(g, core, T, topo, mid, rank, i):
    n, e, w, via = SETS[i]
    tr = []
    for b, (j, c0, _) in enumerate(blocks()):
        if j == i:
            es = engines(topo, core, mid[b])[len(tr) * e:(len(tr) + 1) * e]
            tr.append(transfer(topo, core, mid[b], es, T.sem.din, T.xr[:, c0:c0 + w], T.slots[:, rank * w:(rank + 1) * w]))
    g.remote_dma_fused(tr, local_sem=T.sem.ls)
    return n * e


def rank_part(g, core, T, topo, mid, rank):
    S, V, A = T.sem, g.vector, AluOpType
    g.scalar.dma_start(T.hb[:], T.hh[:]).then_inc(S.ldh, 16)
    g.sync.dma_start(T.xs[:], T.x[:]).then_inc(S.ldx, 16)

    nc = COLS // 16
    g.iota(T.pi[:], [[0, 1]], 0, 1).then_inc(S.iot, 1)
    g.iota(T.i2[:], [[16, nc]], 0, 0).then_inc(S.iot, 1)
    g.wait_ge(S.ldh, 16)
    g.partition_broadcast(T.hbc[:], T.hb[0:1, 0:1], 128).then_inc(S.bc, 1)

    V.wait_ge(S.iot, 2)
    V.tensor_scalar(T.pm[:], T.pi[:], 15, None, A.bitwise_and).then_inc(S.vq, 1)
    V.wait_ge(S.vq, 1)
    V.tensor_copy(T.pf[:], T.pm[:]).then_inc(S.vq, 1)
    V.wait_ge(S.vq, 2)
    V.tensor_scalar(T.base[:], T.i2[:], T.pf[:], None, A.add).then_inc(S.vq, 1)
    V.wait_ge(S.bc, 1)
    V.tensor_scalar(T.hi[:, 1:2], T.hbc[:], COLS - 1, None, A.bitwise_and).then_inc(S.vq, 1)
    V.tensor_scalar(T.hi[:, 0:1], T.hbc[:], 12, None, A.arith_shift_right).then_inc(S.vq, 1)
    V.tensor_copy(T.hw[:], T.hbc[:]).then_inc(S.vq, 1)
    V.wait_ge(S.vq, 6)
    V.tensor_copy(T.hf[:], T.hi[:]).then_inc(S.hrdy, 1)
    cut = span(0)[1] // 16
    two = ((0, cut), (cut, nc))
    for a, z in two:
        V.tensor_scalar(T.i1[:, a:z], T.base[:, a:z], T.hw[:], None, A.add).then_inc(S.vq, 1)
    V.wait_ge(S.vq, 8)
    for a, z in two:
        V.tensor_scalar(T.i2[:, a:z], T.i1[:, a:z], COLS - 1, None, A.bitwise_and).then_inc(S.vq, 1)
    V.wait_ge(S.vq, 10)
    for (a, z), sem in zip(two, (S.la, S.lb)):
        V.tensor_copy(T.lst[:, a:z], T.i2[:, a:z]).then_inc(sem, 1)

    for q in (V, g.scalar):
        q.wait_ge(S.la, 1)
        q.wait_ge(S.ldx, 16)
    for i in range(len(SETS)):
        if i == 1:
            V.wait_ge(S.lb, 1)
            g.scalar.wait_ge(S.lb, 1)
        lo, hi = span(i)
        mi = (lo + hi) // 2
        V.tensor_copy(T.xr[:, lo:mi], T.xs[:].indirect(T.lst[:, lo // 16:mi // 16])).then_inc(S["c%d" % i], 1)
        g.scalar.activation(T.xr[:, mi:hi], T.xs[:].indirect(T.lst[:, mi // 16:hi // 16]),
                            ActivationFunctionType.Copy, bias=-0.0).then_inc(S["c%d" % i], 1)

    g.wait_ge(S.hrdy, 1)
    tr, mine = [], parts_of(rank, mid)
    k = 8 // len(mine)
    for n in mine:
        es = engines(topo, core, mid[n])[len(tr) * k:(len(tr) + 1) * k]
        col = n % 2
        tr.append(transfer(topo, core, mid[n], es, S.hr, T.hf[:, col:col + 1], T.hf[:, col:col + 1]))
    g.remote_dma_fused(tr, local_sem=S.ls)
    total = 8

    helpers = helpers_of(core, mid, topo)
    off = engines(topo, core, mid[0])
    for i, (n, e, w, via) in enumerate(SETS):
        g.wait_ge(S["c%d" % i], 2)
        if via is None:
            total += send_set(g, core, T, topo, mid, rank, i)
        else:
            es = [x for x in engines(topo, core, helpers[via]) if x not in off]
            lo, hi = span(i)
            g.remote_dma_fused([transfer(topo, core, helpers[via], es, S["hop%d" % i], T.xr[:, lo:hi], T.xr[:, lo:hi])],
                               local_sem=S.ls)
            total += len(es)

    for name, first, last in STORES:
        q, st = (g.scalar, S.stb) if name == "scalar" else (g.sync, S.sta)
        for i in range(first, last):
            q.wait_ge(S["z%d" % i], sum(dict(send_list(b))[rank] for b, (j, c0, w) in enumerate(blocks()) if j == i))
        lo, hi = span(first)[0], span(last - 1)[1]
        q.dma_start(T.y[:, lo:hi], T.z[:, lo:hi]).then_inc(st, 16)
    g.sync.wait_ge(S.sta, 32)
    g.scalar.wait_ge(S.stb, 32)
    g.wait_ge(S.ls, total)


def helper_part(g, core, T, topo, mid, rank, k):
    off = engines(topo, T.cores[rank], mid[0])
    es = [x for x in engines(topo, T.cores[rank], core) if x not in off]
    total = 0
    for i in range(len(SETS)):
        if SETS[i][3] == k:
            g.wait_ge(T.sem["hop%d" % i], len(es))
            total += send_set(g, core, T, topo, mid, rank, i)
    g.wait_ge(T.sem.ls, total)


def middle_part(g, core, T, topo, mid, b):
    S, V, A = T.sem, g.vector, AluOpType
    i, c0, w = blocks()[b]
    n, nc, wc = N * w, N * w // 16, w // 16
    order = send_list(b)
    first = order[0][0]
    g.iota(T.pi[:], [[0, 1]], 0, 1).then_inc(S.iot, 1)
    g.iota(T.f1[:, 0:(N - first) * wc], [[16, (N - first) * wc]], first * w, 0,
           allow_small_or_imprecise_dtypes=True).then_inc(S.iot, 1)
    k = 2
    if first:
        g.iota(T.f1[:, (N - first) * wc:nc], [[16, first * wc]], 0, 0,
               allow_small_or_imprecise_dtypes=True).then_inc(S.iot, 1)
        k += 1
    g.iota(T.f2[:, 0:nc], [[0, N], [16, wc]], c0, 0, allow_small_or_imprecise_dtypes=True).then_inc(S.iot, 1)
    k += 1

    col = b % 2
    peer = mid[b ^ 1]
    direct = 8 // len(parts_of((b // 2) % N, mid))
    g.wait_ge(S.hr, direct)
    g.remote_dma_fused([transfer(topo, core, peer, engines(topo, core, peer), S.hm,
                                 T.hf[:, col:col + 1], T.hf[:, col:col + 1])], local_sem=S.ls)

    base, pos, f1, f2, f3 = (t[:, 0:nc] for t in (T.base, T.pos, T.f1, T.f2, T.f3))
    q, s = T.hf[:, 0:1], T.hf[:, 1:2]
    count = [0]

    def step(ins):
        ins.then_inc(S.vq, 1)
        count[0] += 1
        V.wait_ge(S.vq, count[0])

    V.wait_ge(S.iot, k)
    step(V.tensor_scalar(T.pm[:], T.pi[:], 15, None, A.bitwise_and))
    step(V.tensor_copy(T.pf[:], T.pm[:]))
    step(V.tensor_scalar(base, f1, T.pf[:], None, A.add))
    step(V.tensor_scalar(pos, f2, T.pf[:], None, A.add))
    V.wait_ge(S.hr, direct)
    if col == 0:
        step(V.tensor_scalar(T.qw[:], q, float(w), None, A.mult))
        step(V.tensor_scalar(f1, base, T.qw[:], None, A.add))
        step(V.tensor_scalar(f2, f1, float(n), float(-n), A.is_ge, A.mult))
        step(V.tensor_tensor(f3, f1, f2, A.add))
        step(V.tensor_scalar(f1, f3, float(n - w), float(-n), A.is_ge, A.mult))
        step(V.tensor_scalar(base, f1, float(w), None, A.add))
        V.wait_ge(S.hm, len(engines(topo, peer, core)))
        step(V.tensor_scalar(f2, pos, s, float(COLS), A.add, A.is_ge))
        step(V.tensor_tensor(f1, f2, base, A.mult))
        step(V.tensor_tensor(pos, f1, f3, A.add))
    else:
        step(V.tensor_scalar(f1, pos, s, float(COLS), A.add, A.is_ge))
        step(V.tensor_scalar(f2, f1, float(w), None, A.mult))
        step(V.tensor_tensor(f3, base, f2, A.add))
        V.wait_ge(S.hm, len(engines(topo, peer, core)))
        step(V.tensor_scalar(T.qw[:], q, float(w), None, A.mult))
        step(V.tensor_scalar(f1, f3, T.qw[:], None, A.add))
        step(V.tensor_scalar(f2, f1, float(n), float(-n), A.is_ge, A.mult))
        step(V.tensor_tensor(pos, f1, f2, A.add))
    V.tensor_copy(T.lst[:, 0:nc], pos).then_inc(S.la, 1)

    got = N * SETS[i][1]
    for qu in (V, g.scalar):
        qu.wait_ge(S.la, 1)
        qu.wait_ge(S.din, got)
    win = T.slots[:, 0:n]
    lo = 0
    for k, (m, e) in enumerate(SPLIT):
        mi, hi = lo + m // 2, lo + m
        V.tensor_copy(T.res[:, lo * w:mi * w], win.indirect(T.lst[:, lo * wc:mi * wc])).then_inc(S["c%d" % k], 1)
        g.scalar.activation(T.res[:, mi * w:hi * w], win.indirect(T.lst[:, mi * wc:hi * wc]),
                            ActivationFunctionType.Copy, bias=-0.0).then_inc(S["c%d" % k], 1)
        g.wait_ge(S["c%d" % k], 2)
        tr = []
        for t in range(lo, hi):
            r, e = order[t]
            dst = T.cores[r]
            tr.append(transfer(topo, core, dst, engines(topo, core, dst)[len(tr) * e:(len(tr) + 1) * e], S["z%d" % i],
                               T.res[:, t * w:(t + 1) * w], T.z[:, c0:c0 + w]))
        g.remote_dma_fused(tr, local_sem=S.ls)
        lo = hi
    g.wait_ge(S.ls, len(engines(topo, core, peer)) + sum(m * e for m, e in SPLIT))


def rank_program(g, core, T, topo):
    mid = place(T.cores, topo)
    rank = T.rank_of(core)
    if rank is not None:
        rank_part(g, core, T, topo, mid, rank)
    elif core in mid:
        middle_part(g, core, T, topo, mid, mid.index(core))
    else:
        for r, rcore in enumerate(T.cores):
            helpers = helpers_of(rcore, mid, topo)
            if core in helpers:
                helper_part(g, core, T, topo, mid, r, helpers.index(core))
